import numpy as np
import ml_dtypes


def mxq(x, axis, fmt="e4m3"):
    dtype, down = {"e4m3": (ml_dtypes.float8_e4m3fn, 7), "e5m2": (ml_dtypes.float8_e5m2, 14)}[fmt]
    v = np.moveaxis(np.asarray(x, np.float32).astype(ml_dtypes.bfloat16).astype(np.float64), axis, -1)
    blocks = v.reshape(v.shape[:-1] + (-1, 32))
    amax = np.abs(blocks).max(-1, keepdims=True)
    byte = np.maximum(np.where(amax > 0, np.frexp(amax)[1] - 1 + 127, 0) - down, 1)
    scale = np.exp2(byte - 127.0)
    codes = (blocks / scale).astype(np.float32).astype(dtype).astype(np.float64)
    return np.moveaxis((codes * scale).reshape(v.shape), -1, axis)


WIDE = False


def mx_kscale(k):
    if not WIDE:
        return np.ones(k)
    levels = np.array([10, -10, 5, -5, 0])
    if k % 512:
        return np.exp2(np.random.permutation(np.resize(levels, k // 32))).repeat(32)
    a = np.empty((k // 512, 16))
    for p in range(k // 512):
        a[p, :8] = np.random.permutation(np.resize(levels, 8))
        for g in range(8):
            far = levels[np.abs(levels - a[p, g]) >= 10]
            a[p, g + 8] = far[np.random.randint(len(far))]
    return np.exp2(a.ravel()).repeat(32)


def f64(x):
    return np.asarray(x).astype(np.float64)


def striped(idx):
    return np.tile(idx.reshape(-1, 16).T, (8, 1)).astype(np.uint16)


def unstriped(offs):
    return offs[:16].T.reshape(-1).astype(np.int64)


def striped8(idx):
    return np.concatenate([x.reshape(-1, 16).T for x in idx]).astype(np.uint16)


def runs(offs, k):
    lists = np.stack([offs[16 * r : 16 * r + 16].T.reshape(-1) for r in range(8)]).astype(np.int64)
    return lists[np.arange(k) % 512 // 64]


def pack_weight(w):
    k, n = w.shape
    w = f64(np.asarray(w, np.float32).astype(ml_dtypes.bfloat16)).reshape(k // 32, 32, n)
    amax = np.abs(w).max(1)
    byte = np.clip(np.where(amax > 0, np.frexp(amax)[1] - 1 + 127 - 7, 1), 1, 254)
    scaled = (w * np.exp2(127.0 - byte)[:, None, :]).reshape(k, n).astype(np.float32)
    words = np.ascontiguousarray(scaled.reshape(k // 512, 128, 4, n).transpose(0, 1, 3, 2)).astype(ml_dtypes.float8_e4m3fn).view(np.uint8)
    return words, np.ascontiguousarray(byte.astype(np.uint8).reshape(k // 512, 16, n))


def unpack_weight(words, scales):
    g, p, n, _ = words.shape
    vals = np.ascontiguousarray(words).view(ml_dtypes.float8_e4m3fn).astype(np.float64) * np.repeat(np.exp2(scales.astype(np.float64) - 127.0), 8, axis=1)[..., None]
    return vals.transpose(0, 1, 3, 2).reshape(g * 512, n)


E2M1 = np.array([0.0, 0.5, 1.0, 1.5, 2.0, 3.0, 4.0, 6.0, -0.0, -0.5, -1.0, -1.5, -2.0, -3.0, -4.0, -6.0])


def pack_fp4(w):
    k, n = w.shape
    w = f64(np.asarray(w, np.float32).astype(ml_dtypes.bfloat16)).reshape(k // 32, 32, n)
    amax = np.abs(w).max(1)
    mant, ex = np.frexp(amax / 6.0)
    byte = np.clip(np.where(amax > 0, np.where(mant > 0.5, ex, ex - 1) + 127, 1), 1, 254)
    scaled = (w * np.exp2(127.0 - byte)[:, None, :]).reshape(k, n).astype(np.float32)
    c = np.ascontiguousarray(scaled.reshape(k // 512, 128, 4, n).transpose(0, 1, 3, 2)).astype(ml_dtypes.float4_e2m1fn).view(np.uint8) & 0xF
    words = (c[..., 0::2] | (c[..., 1::2] << 4)).reshape(k // 512, 128, 2 * n)
    return np.ascontiguousarray(words), np.ascontiguousarray(byte.astype(np.uint8).reshape(k // 512, 16, n))


def unpack_fp4(words, scales):
    g, _, n = scales.shape
    words = np.ascontiguousarray(words).reshape(g, 128, n, 2)
    nib = np.empty((g, 128, n, 4), np.uint8)
    nib[..., 0::2] = words & 0xF
    nib[..., 1::2] = words >> 4
    vals = E2M1[nib] * np.repeat(np.exp2(scales.astype(np.float64) - 127.0), 8, axis=1)[..., None]
    return vals.transpose(0, 1, 3, 2).reshape(g * 512, n)


def sigmoid(v):
    return 1.0 / (1.0 + np.exp(-np.maximum(v, -700.0)))


K, T, S, H, G = 512, 1024, 256, 512, 2048


def setup_inputs():
    n = np.random.standard_normal
    s = mx_kscale(K)[:, None]
    packed_xT = pack_weight(n((K, T)) * s)
    packed_w1 = pack_fp4(n((K, H)) / np.sqrt(K) / s)
    packed_dT = pack_weight(n((K, G)) / s)
    return {
        "x_words": packed_xT[0],
        "x_scales": packed_xT[1],
        "w1_words": packed_w1[0],
        "w1_scales": packed_w1[1],
        "sl": np.random.uniform(1.5, 3.0, (H, 1)).astype(np.float32),
        "th": (0.5 * n((H, 1))).astype(np.float32),
        "gs": (np.random.uniform(0.5, 1.5, (K, 1)) * s).astype(np.float32),
        "d_words": packed_dT[0],
        "d_scales": packed_dT[1],
        "offs": striped(np.random.permutation(T)[:S]),
        "n1": striped8(np.stack([np.random.permutation(S) for _ in range(8)])),
        "n2": striped8(np.stack([np.random.permutation(S) for _ in range(8)])),
        "k1": striped8(np.random.randint(0, G, (8, H))),
        "k2": striped8(np.random.randint(0, G, (8, H))),
        "two": striped(np.random.permutation(T)[:S]),
        "n3": striped(np.random.permutation(S)),
    }


def reference(x_words, x_scales, w1_words, w1_scales, sl, th, gs, d_words, d_scales, offs, n1, n2, k1, k2, two, n3):
    d_k1 = unpack_weight(d_words, d_scales)[np.arange(K)[:, None], runs(k1, K)]
    xq = unpack_weight(x_words, x_scales)[:, unstriped(offs)]
    y = unpack_fp4(w1_words, w1_scales).T @ xq
    sg = sigmoid(f64(sl) * (y[np.arange(H)[:, None], runs(n1, H)] - f64(th)))
    z = f64(gs) * (1.5 * (y * (sg - (sg[np.arange(H)[:, None], runs(n2, H)]))))
    d_k2 = unpack_weight(d_words, d_scales)[np.arange(K)[:, None], runs(k2, K)]
    x_two = unpack_weight(x_words, x_scales)[:, unstriped(two)]
    h = 0.0625 * ((d_k1.T @ mxq(z, 0, "e4m3") + d_k2.T @ x_two))
    ds = np.zeros((H, S))
    ds[:, unstriped(n3)] = h
    return h - ds

@@ -1,0 +1,213 @@
+from contextlib import ExitStack
+
+import concourse.mybir as mybir
+
+K, T, S, H, G = 512, 1024, 256, 512, 2048
+P = 128
+HALF = S // 2
+FLOPS = 3 * 2 * K * H * S
+
+F32 = mybir.dt.float32
+BF16 = mybir.dt.bfloat16
+I32 = mybir.dt.int32
+U32 = mybir.dt.uint32
+U16 = mybir.dt.uint16
+U8 = mybir.dt.uint8
+FP8X4 = mybir.dt.float8_e4m3fn_x4
+FP4X4 = mybir.dt.float4_e2m1fn_x4
+ALU = mybir.AluOpType
+ACT = mybir.ActivationFunctionType
+
+
+def entries(lists, first, count):
+    return lists[:, first // 16 : (first + count) // 16]
+
+
+def tile_picked_cmixedbsendmx_none_p_kernel(
+    tc, x_words, x_scales, w1_words, w1_scales, sl, th, gs, d_words, d_scales, offs, n1, n2, k1, k2, two, n3, out
+):
+    nc = tc.nc
+    with ExitStack() as ctx:
+        pool = ctx.enter_context(tc.tile_pool(name="held", bufs=1))
+        psum = ctx.enter_context(tc.psum_pool(name="psum", bufs=1))
+
+        def sbuf(name, shape, dtype):
+            return pool.tile(shape, dtype, name=name, align_bytes=64)
+
+        def load_list(name, source):
+            tile = pool.tile([P, source.shape[1]], U16, name=name)
+            nc.sync.dma_start(tile[:], source)
+            return tile
+
+        def load_column(name, source, queue):
+            tile = sbuf(name, [P, 4], F32)
+            queue.dma_start(tile[:], source.rearrange("(p t) o -> p (t o)", t=4))
+            return tile
+
+        x_scale_table = sbuf("x_scale_table", [P, T], U8)
+        w1_scale_raw = sbuf("w1_scale_raw", [P, H], U8)
+        d_scale_table = sbuf("d_scale_table", [P, G], U8)
+        placed = sbuf("d_placed_scales", [P, 2 * H], U8)
+        for tile in (x_scale_table, w1_scale_raw, placed):
+            nc.vector.memset(tile[:].bitcast(I32), 0)
+        nc.gpsimd.memset(d_scale_table[:].bitcast(I32), 0)
+
+        x_word_table = sbuf("x_word_table", [P, T], I32)
+        nc.sync.dma_start(x_word_table[:], x_words[0].rearrange("p n t -> p (n t)").bitcast(I32))
+        offs_list = load_list("offs_list", offs)
+        w1_raw = sbuf("w1_raw", [P, 2 * H], U8)
+        nc.sync.dma_start(w1_raw[:].bitcast(I32), w1_words[0].bitcast(I32))
+        for q in range(4):
+            nc.scalar.dma_start(
+                x_scale_table[32 * q : 32 * q + 4, :].bitcast(I32), x_scales[0, 4 * q : 4 * q + 4, :].bitcast(I32)
+            )
+        for q in range(4):
+            queue = nc.sync
+            queue.dma_start(
+                w1_scale_raw[32 * q : 32 * q + 4, :].bitcast(I32), w1_scales[0, 4 * q : 4 * q + 4, :].bitcast(I32)
+            )
+        n1_list = load_list("n1_list", n1)
+        slope = load_column("slope", sl, nc.sync)
+        threshold = load_column("threshold", th, nc.sync)
+        k1_list = load_list("k1_list", k1)
+        k2_list = load_list("k2_list", k2)
+        for e in range(2):
+            nc.gpsimd.dma_start(d_scale_table[e:P:16, :].bitcast(I32), d_scales[0, e:16:2, :].bitcast(I32))
+        d_word_table = sbuf("d_word_table", [P, G], I32)
+        nc.sync.dma_start(d_word_table[:], d_words[0].rearrange("p n t -> p (n t)").bitcast(I32))
+        two_list = load_list("two_list", two)
+        n2_list = load_list("n2_list", n2)
+        gain = load_column("gain", gs, nc.gpsimd)
+        n3_list = load_list("n3_list", n3)
+
+        def gather(out_ap, table, offsets):
+            nc.vector.tensor_copy(out_ap, table.indirect(offsets))
+
+        w1_dealt = sbuf("w1_dealt", [P, 2 * H], U8)
+        nc.scalar.copy(
+            w1_dealt[:].bitcast(U16).rearrange("p (t m) -> p t m", t=4),
+            w1_raw[:].bitcast(U16).rearrange("p (m t) -> p t m", t=4),
+        )
+        xq_scales = sbuf("xq_scales", [P, S], U8)
+        gather(xq_scales[:], x_scale_table[:], offs_list[:])
+        w1_scale_dealt = sbuf("w1_scale_dealt", [P, H], U8)
+        nc.vector.tensor_copy(
+            w1_scale_dealt[:].rearrange("p (t m) -> p t m", t=4),
+            w1_scale_raw[:].rearrange("p (m t) -> p t m", t=4),
+        )
+        xq_words = sbuf("xq_words", [P, S], U32)
+        gather(xq_words[:], x_word_table[:].bitcast(U32), offs_list[:])
+
+        bias = sbuf("bias", [P, 4], F32)
+        nc.vector.scalar_tensor_tensor(bias[:], threshold[:], -1.0, slope[:], ALU.mult, ALU.mult)
+
+        y, sg = [], []
+        for t in range(4):
+            bank = psum.tile([P, S], F32, name=f"y_bank{t}", tag=f"bank{t}")
+            nc.tensor.matmul_mx(
+                out=bank[:],
+                lhsT=w1_dealt[:, 2 * P * t : 2 * P * (t + 1)].bitcast(FP4X4),
+                lhsT_scale=w1_scale_dealt[:, P * t : P * (t + 1)],
+                rhs=xq_words[:].bitcast(FP8X4),
+                rhs_scale=xq_scales[:],
+                start=True,
+                stop=True,
+            )
+            y.append(sbuf(f"y{t}", [P, 2 * S], F32))
+            nc.scalar.copy(y[t][:, :S], bank[:])
+            sg.append(sbuf(f"sg{t}", [P, S], F32))
+            nc.scalar.activation(
+                sg[t][:], y[t][:].indirect(n1_list[:]), ACT.Sigmoid, bias=bias[:, t : t + 1], scale=slope[:, t : t + 1]
+            )
+
+        xt_scales = sbuf("xt_scales", [P, S], U8)
+        gather(xt_scales[:], x_scale_table[:], two_list[:])
+        xt_words = sbuf("xt_words", [P, S], U32)
+        gather(xt_words[:], x_word_table[:].bitcast(U32), two_list[:])
+        gain15 = sbuf("gain15", [P, 4], F32)
+        nc.vector.tensor_scalar(gain15[:], gain[:], 1.5, None, ALU.mult)
+
+        picked = sbuf("d_picked_scales", [P, 2 * H], U8)
+        for u, lists in enumerate((k1_list, k2_list)):
+            gather(picked[:, H * u : H * (u + 1)], d_scale_table[:], lists[:])
+        for odd in range(2):
+            for e in range(2):
+                nc.sync.dma_start(
+                    placed[2 * odd + e : P : 32, :].bitcast(I32), picked[16 * odd + e : P : 32, :].bitcast(I32)
+                )
+
+        def gather_dictionary(pair):
+            words = []
+            for u, lists in enumerate((k1_list, k2_list)):
+                words.append(sbuf(f"d_picked_words{pair}_{u}", [P, 2 * P], U32))
+                gather(words[u][:], d_word_table[:].bitcast(U32), entries(lists, 2 * P * pair, 2 * P))
+            return words
+
+        z_codes = sbuf("z_codes", [P, S], U32)
+        z_scales = sbuf("z_scales", [P, S], U8)
+
+        def make_z(half):
+            cols = slice(HALF * half, HALF * (half + 1))
+            fetched = sbuf(f"fetched{half}", [P, 4, HALF], F32)
+            diff = sbuf(f"diff{half}", [P, 4, HALF], F32)
+            planes = sbuf(f"planes{half}", [P, 4, HALF], BF16)
+            woven = sbuf(f"woven{half}", [P, HALF, 4], BF16)
+            for t in range(4):
+                nc.scalar.activation(fetched[:, t, :], sg[t][:].indirect(entries(n2_list, HALF * half, HALF)), ACT.Copy)
+                nc.vector.tensor_tensor(diff[:, t, :], sg[t][:, cols], fetched[:, t, :], ALU.subtract)
+                nc.vector.scalar_tensor_tensor(
+                    planes[:, t, :], diff[:, t, :], gain15[:, t : t + 1], y[t][:, cols], ALU.mult, ALU.mult
+                )
+            nc.vector.tensor_copy(
+                woven[:].rearrange("p (c i) t -> p c t i", i=4), planes[:].rearrange("p t (c i) -> p c t i", i=4)
+            )
+            nc.vector.quantize_mx(
+                out=z_codes[:, cols].bitcast(FP8X4), scales=z_scales[:, cols], in_=woven[:].rearrange("p c t -> p (c t)")
+            )
+
+        h = [sbuf(f"h{m}", [P, S], F32) for m in range(4)]
+        sent = [sbuf(f"sent{m}", [P, S if m < 2 else 2 * S], F32) for m in range(4)]
+
+        def make_h(m, first, count, tag, words):
+            cols = slice(first, first + count)
+            mcols = slice(P * (m % 2), P * (m % 2 + 1))
+            bank = psum.tile([P, count], F32, name=f"h_bank{m}_{first}", tag=tag)
+            nc.tensor.matmul_mx(
+                out=bank[:],
+                lhsT=words[1][:, mcols].bitcast(FP8X4),
+                lhsT_scale=placed[:, H + P * m : H + P * (m + 1)],
+                rhs=xt_words[:, cols].bitcast(FP8X4),
+                rhs_scale=xt_scales[:, cols],
+                start=True,
+                stop=False,
+            )
+            nc.tensor.matmul_mx(
+                out=bank[:],
+                lhsT=words[0][:, mcols].bitcast(FP8X4),
+                lhsT_scale=placed[:, P * m : P * (m + 1)],
+                rhs=z_codes[:, cols].bitcast(FP8X4),
+                rhs_scale=z_scales[:, cols],
+                start=False,
+                stop=True,
+            )
+            nc.vector.tensor_scalar(h[m][:, cols], bank[:], 0.0625, None, ALU.mult)
+            nc.scalar.activation(sent[m][:].indirect(entries(n3_list, first, count)), h[m][:, cols], ACT.Copy)
+
+        def finish(m):
+            result = sbuf(f"result{m}", [P, S], F32)
+            nc.vector.tensor_tensor(result[:], h[m][:], sent[m][:, :S], ALU.subtract)
+            nc.sync.dma_start(out[P * m : P * (m + 1), :], result[:])
+
+        low = gather_dictionary(0)
+        make_z(0)
+        make_h(0, 0, HALF, "bank4", low)
+        make_h(1, 0, HALF, "bank5", low)
+        make_z(1)
+        make_h(0, HALF, HALF, "bank6", low)
+        make_h(1, HALF, HALF, "bank7", low)
+        finish(0)
+        finish(1)
+        high = gather_dictionary(1)
+        for m in (2, 3):
+            make_h(m, 0, S, f"bank{m}", high)
+            finish(m)

@@ -66,6 +66,9 @@ def tile_picked_cmixedbsendmx_none_p_kernel(
             queue.dma_start(
                 w1_scale_raw[32 * q : 32 * q + 4, :].bitcast(I32), w1_scales[0, 4 * q : 4 * q + 4, :].bitcast(I32)
             )
+        warm = sbuf("warm", [P, 2], F32)
+        nc.vector.memset(warm[:, 0:1], 0.0)
+        nc.scalar.activation(warm[:, 1:2], warm[:, 0:1], ACT.Sigmoid)
         n1_list = load_list("n1_list", n1)
         slope = load_column("slope", sl, nc.sync)
         threshold = load_column("threshold", th, nc.sync)

@@ -31,8 +31,8 @@ def tile_picked_cmixedbsendmx_none_p_kernel(
         pool = ctx.enter_context(tc.tile_pool(name="held", bufs=1))
         psum = ctx.enter_context(tc.psum_pool(name="psum", bufs=1))
 
-        def sbuf(name, shape, dtype):
-            return pool.tile(shape, dtype, name=name, align_bytes=64)
+        def sbuf(name, shape, dtype, tag=None):
+            return pool.tile(shape, dtype, name=name, tag=tag or name, align_bytes=64)
 
         def load_list(name, source):
             tile = pool.tile([P, source.shape[1]], U16, name=name)
@@ -48,9 +48,8 @@ def tile_picked_cmixedbsendmx_none_p_kernel(
         w1_scale_raw = sbuf("w1_scale_raw", [P, H], U8)
         d_scale_table = sbuf("d_scale_table", [P, G], U8)
         placed = sbuf("d_placed_scales", [P, 2 * H], U8)
-        for tile in (x_scale_table, w1_scale_raw, placed):
+        for tile in (x_scale_table, w1_scale_raw, d_scale_table, placed):
             nc.vector.memset(tile[:].bitcast(I32), 0)
-        nc.gpsimd.memset(d_scale_table[:].bitcast(I32), 0)
 
         x_word_table = sbuf("x_word_table", [P, T], I32)
         nc.sync.dma_start(x_word_table[:], x_words[0].rearrange("p n t -> p (n t)").bitcast(I32))
@@ -72,13 +71,12 @@ def tile_picked_cmixedbsendmx_none_p_kernel(
         n1_list = load_list("n1_list", n1)
         slope = load_column("slope", sl, nc.sync)
         threshold = load_column("threshold", th, nc.sync)
+        nc.sync.dma_start(d_scale_table[0:P:8, :].bitcast(I32), d_scales[0].bitcast(I32))
         k1_list = load_list("k1_list", k1)
         k2_list = load_list("k2_list", k2)
-        for e in range(2):
-            nc.gpsimd.dma_start(d_scale_table[e:P:16, :].bitcast(I32), d_scales[0, e:16:2, :].bitcast(I32))
+        two_list = load_list("two_list", two)
         d_word_table = sbuf("d_word_table", [P, G], I32)
         nc.sync.dma_start(d_word_table[:], d_words[0].rearrange("p n t -> p (n t)").bitcast(I32))
-        two_list = load_list("two_list", two)
         n2_list = load_list("n2_list", n2)
         gain = load_column("gain", gs, nc.gpsimd)
         n3_list = load_list("n3_list", n3)
@@ -133,16 +131,13 @@ def tile_picked_cmixedbsendmx_none_p_kernel(
         picked = sbuf("d_picked_scales", [P, 2 * H], U8)
         for u, lists in enumerate((k1_list, k2_list)):
             gather(picked[:, H * u : H * (u + 1)], d_scale_table[:], lists[:])
-        for odd in range(2):
-            for e in range(2):
-                nc.sync.dma_start(
-                    placed[2 * odd + e : P : 32, :].bitcast(I32), picked[16 * odd + e : P : 32, :].bitcast(I32)
-                )
+        for j in range(4):
+            nc.sync.dma_start(placed[j:P:32, :].bitcast(I32), picked[8 * j : P : 32, :].bitcast(I32))
 
         def gather_dictionary(pair):
             words = []
             for u, lists in enumerate((k1_list, k2_list)):
-                words.append(sbuf(f"d_picked_words{pair}_{u}", [P, 2 * P], U32))
+                words.append(sbuf(f"d_picked_words{pair}_{u}", [P, 2 * P], U32, tag="woven1" if (pair, u) == (1, 0) else None))
                 gather(words[u][:], d_word_table[:].bitcast(U32), entries(lists, 2 * P * pair, 2 * P))
             return words
 
@@ -158,6 +153,7 @@ def tile_picked_cmixedbsendmx_none_p_kernel(
             for t in range(4):
                 nc.scalar.activation(fetched[:, t, :], sg[t][:].indirect(entries(n2_list, HALF * half, HALF)), ACT.Copy)
                 nc.vector.tensor_tensor(diff[:, t, :], sg[t][:, cols], fetched[:, t, :], ALU.subtract)
+            for t in range(4):
                 nc.vector.scalar_tensor_tensor(
                     planes[:, t, :], diff[:, t, :], gain15[:, t : t + 1], y[t][:, cols], ALU.mult, ALU.mult
                 )
@@ -193,13 +189,18 @@ def tile_picked_cmixedbsendmx_none_p_kernel(
                 start=False,
                 stop=True,
             )
-            nc.vector.tensor_scalar(h[m][:, cols], bank[:], 0.0625, None, ALU.mult)
+            if m < 2 and first == 0:
+                nc.scalar.mul(h[m][:, cols], bank[:], 0.0625)
+            else:
+                nc.vector.tensor_scalar(h[m][:, cols], bank[:], 0.0625, None, ALU.mult)
             nc.scalar.activation(sent[m][:].indirect(entries(n3_list, first, count)), h[m][:, cols], ACT.Copy)
 
         def finish(m):
             result = sbuf(f"result{m}", [P, S], F32)
-            nc.vector.tensor_tensor(result[:], h[m][:], sent[m][:, :S], ALU.subtract)
-            nc.sync.dma_start(out[P * m : P * (m + 1), :], result[:])
+            pieces = ((0, S, nc.sync),) if m < 3 else ((0, HALF, nc.sync), (HALF, S, nc.scalar))
+            for first, last, queue in pieces:
+                nc.vector.tensor_tensor(result[:, first:last], h[m][:, first:last], sent[m][:, first:last], ALU.subtract)
+                queue.dma_start(out[P * m : P * (m + 1), first:last], result[:, first:last])
 
         low = gather_dictionary(0)
         make_z(0)
@@ -208,9 +209,9 @@ def tile_picked_cmixedbsendmx_none_p_kernel(
         make_z(1)
         make_h(0, HALF, HALF, "bank6", low)
         make_h(1, HALF, HALF, "bank7", low)
+        high = gather_dictionary(1)
         finish(0)
         finish(1)
-        high = gather_dictionary(1)
         for m in (2, 3):
             make_h(m, 0, S, f"bank{m}", high)
             finish(m)

from contextlib import ExitStack

import concourse.mybir as mybir

K, T, S, H, G = 512, 1024, 256, 512, 2048
P = 128
HALF = S // 2
FLOPS = 3 * 2 * K * H * S

F32 = mybir.dt.float32
BF16 = mybir.dt.bfloat16
I32 = mybir.dt.int32
U32 = mybir.dt.uint32
U16 = mybir.dt.uint16
U8 = mybir.dt.uint8
FP8X4 = mybir.dt.float8_e4m3fn_x4
FP4X4 = mybir.dt.float4_e2m1fn_x4
ALU = mybir.AluOpType
ACT = mybir.ActivationFunctionType


def entries(lists, first, count):
    return lists[:, first // 16 : (first + count) // 16]


def tile_picked_cmixedbsendmx_none_p_kernel(
    tc, x_words, x_scales, w1_words, w1_scales, sl, th, gs, d_words, d_scales, offs, n1, n2, k1, k2, two, n3, out
):
    nc = tc.nc
    with ExitStack() as ctx:
        pool = ctx.enter_context(tc.tile_pool(name="held", bufs=1))
        psum = ctx.enter_context(tc.psum_pool(name="psum", bufs=1))

        def sbuf(name, shape, dtype, tag=None):
            return pool.tile(shape, dtype, name=name, tag=tag or name, align_bytes=64)

        def load_list(name, source):
            tile = pool.tile([P, source.shape[1]], U16, name=name)
            nc.sync.dma_start(tile[:], source)
            return tile

        def load_column(name, source, queue):
            tile = sbuf(name, [P, 4], F32)
            queue.dma_start(tile[:], source.rearrange("(p t) o -> p (t o)", t=4))
            return tile

        x_scale_table = sbuf("x_scale_table", [P, T], U8)
        w1_scale_raw = sbuf("w1_scale_raw", [P, H], U8)
        d_scale_table = sbuf("d_scale_table", [P, G], U8)
        placed = sbuf("d_placed_scales", [P, 2 * H], U8)
        for tile in (x_scale_table, w1_scale_raw, d_scale_table, placed):
            nc.vector.memset(tile[:].bitcast(I32), 0)

        x_word_table = sbuf("x_word_table", [P, T], I32)
        nc.sync.dma_start(x_word_table[:], x_words[0].rearrange("p n t -> p (n t)").bitcast(I32))
        offs_list = load_list("offs_list", offs)
        w1_raw = sbuf("w1_raw", [P, 2 * H], U8)
        nc.sync.dma_start(w1_raw[:].bitcast(I32), w1_words[0].bitcast(I32))
        for q in range(4):
            nc.scalar.dma_start(
                x_scale_table[32 * q : 32 * q + 4, :].bitcast(I32), x_scales[0, 4 * q : 4 * q + 4, :].bitcast(I32)
            )
        for q in range(4):
            queue = nc.sync
            queue.dma_start(
                w1_scale_raw[32 * q : 32 * q + 4, :].bitcast(I32), w1_scales[0, 4 * q : 4 * q + 4, :].bitcast(I32)
            )
        warm = sbuf("warm", [P, 2], F32)
        nc.vector.memset(warm[:, 0:1], 0.0)
        nc.scalar.activation(warm[:, 1:2], warm[:, 0:1], ACT.Sigmoid)
        n1_list = load_list("n1_list", n1)
        slope = load_column("slope", sl, nc.sync)
        threshold = load_column("threshold", th, nc.sync)
        nc.sync.dma_start(d_scale_table[0:P:8, :].bitcast(I32), d_scales[0].bitcast(I32))
        k1_list = load_list("k1_list", k1)
        k2_list = load_list("k2_list", k2)
        two_list = load_list("two_list", two)
        d_word_table = sbuf("d_word_table", [P, G], I32)
        nc.sync.dma_start(d_word_table[:], d_words[0].rearrange("p n t -> p (n t)").bitcast(I32))
        n2_list = load_list("n2_list", n2)
        gain = load_column("gain", gs, nc.gpsimd)
        n3_list = load_list("n3_list", n3)

        def gather(out_ap, table, offsets):
            nc.vector.tensor_copy(out_ap, table.indirect(offsets))

        w1_dealt = sbuf("w1_dealt", [P, 2 * H], U8)
        nc.scalar.copy(
            w1_dealt[:].bitcast(U16).rearrange("p (t m) -> p t m", t=4),
            w1_raw[:].bitcast(U16).rearrange("p (m t) -> p t m", t=4),
        )
        xq_scales = sbuf("xq_scales", [P, S], U8)
        gather(xq_scales[:], x_scale_table[:], offs_list[:])
        w1_scale_dealt = sbuf("w1_scale_dealt", [P, H], U8)
        nc.vector.tensor_copy(
            w1_scale_dealt[:].rearrange("p (t m) -> p t m", t=4),
            w1_scale_raw[:].rearrange("p (m t) -> p t m", t=4),
        )
        xq_words = sbuf("xq_words", [P, S], U32)
        gather(xq_words[:], x_word_table[:].bitcast(U32), offs_list[:])

        bias = sbuf("bias", [P, 4], F32)
        nc.vector.scalar_tensor_tensor(bias[:], threshold[:], -1.0, slope[:], ALU.mult, ALU.mult)

        y, sg = [], []
        for t in range(4):
            bank = psum.tile([P, S], F32, name=f"y_bank{t}", tag=f"bank{t}")
            nc.tensor.matmul_mx(
                out=bank[:],
                lhsT=w1_dealt[:, 2 * P * t : 2 * P * (t + 1)].bitcast(FP4X4),
                lhsT_scale=w1_scale_dealt[:, P * t : P * (t + 1)],
                rhs=xq_words[:].bitcast(FP8X4),
                rhs_scale=xq_scales[:],
                start=True,
                stop=True,
            )
            y.append(sbuf(f"y{t}", [P, 2 * S], F32))
            nc.scalar.copy(y[t][:, :S], bank[:])
            sg.append(sbuf(f"sg{t}", [P, S], F32))
            nc.scalar.activation(
                sg[t][:], y[t][:].indirect(n1_list[:]), ACT.Sigmoid, bias=bias[:, t : t + 1], scale=slope[:, t : t + 1]
            )

        xt_scales = sbuf("xt_scales", [P, S], U8)
        gather(xt_scales[:], x_scale_table[:], two_list[:])
        xt_words = sbuf("xt_words", [P, S], U32)
        gather(xt_words[:], x_word_table[:].bitcast(U32), two_list[:])
        gain15 = sbuf("gain15", [P, 4], F32)
        nc.vector.tensor_scalar(gain15[:], gain[:], 1.5, None, ALU.mult)

        picked = sbuf("d_picked_scales", [P, 2 * H], U8)
        for u, lists in enumerate((k1_list, k2_list)):
            gather(picked[:, H * u : H * (u + 1)], d_scale_table[:], lists[:])
        for j in range(4):
            nc.sync.dma_start(placed[j:P:32, :].bitcast(I32), picked[8 * j : P : 32, :].bitcast(I32))

        def gather_dictionary(pair):
            words = []
            for u, lists in enumerate((k1_list, k2_list)):
                words.append(sbuf(f"d_picked_words{pair}_{u}", [P, 2 * P], U32, tag="woven1" if (pair, u) == (1, 0) else None))
                gather(words[u][:], d_word_table[:].bitcast(U32), entries(lists, 2 * P * pair, 2 * P))
            return words

        z_codes = sbuf("z_codes", [P, S], U32)
        z_scales = sbuf("z_scales", [P, S], U8)

        def make_z(half):
            cols = slice(HALF * half, HALF * (half + 1))
            fetched = sbuf(f"fetched{half}", [P, 4, HALF], F32)
            diff = sbuf(f"diff{half}", [P, 4, HALF], F32)
            planes = sbuf(f"planes{half}", [P, 4, HALF], BF16)
            woven = sbuf(f"woven{half}", [P, HALF, 4], BF16)
            for t in range(4):
                nc.scalar.activation(fetched[:, t, :], sg[t][:].indirect(entries(n2_list, HALF * half, HALF)), ACT.Copy)
                nc.vector.tensor_tensor(diff[:, t, :], sg[t][:, cols], fetched[:, t, :], ALU.subtract)
            for t in range(4):
                nc.vector.scalar_tensor_tensor(
                    planes[:, t, :], diff[:, t, :], gain15[:, t : t + 1], y[t][:, cols], ALU.mult, ALU.mult
                )
            nc.vector.tensor_copy(
                woven[:].rearrange("p (c i) t -> p c t i", i=4), planes[:].rearrange("p t (c i) -> p c t i", i=4)
            )
            nc.vector.quantize_mx(
                out=z_codes[:, cols].bitcast(FP8X4), scales=z_scales[:, cols], in_=woven[:].rearrange("p c t -> p (c t)")
            )

        h = [sbuf(f"h{m}", [P, S], F32) for m in range(4)]
        sent = [sbuf(f"sent{m}", [P, S if m < 2 else 2 * S], F32) for m in range(4)]

        def make_h(m, first, count, tag, words):
            cols = slice(first, first + count)
            mcols = slice(P * (m % 2), P * (m % 2 + 1))
            bank = psum.tile([P, count], F32, name=f"h_bank{m}_{first}", tag=tag)
            nc.tensor.matmul_mx(
                out=bank[:],
                lhsT=words[1][:, mcols].bitcast(FP8X4),
                lhsT_scale=placed[:, H + P * m : H + P * (m + 1)],
                rhs=xt_words[:, cols].bitcast(FP8X4),
                rhs_scale=xt_scales[:, cols],
                start=True,
                stop=False,
            )
            nc.tensor.matmul_mx(
                out=bank[:],
                lhsT=words[0][:, mcols].bitcast(FP8X4),
                lhsT_scale=placed[:, P * m : P * (m + 1)],
                rhs=z_codes[:, cols].bitcast(FP8X4),
                rhs_scale=z_scales[:, cols],
                start=False,
                stop=True,
            )
            if m < 2 and first == 0:
                nc.scalar.mul(h[m][:, cols], bank[:], 0.0625)
            else:
                nc.vector.tensor_scalar(h[m][:, cols], bank[:], 0.0625, None, ALU.mult)
            nc.scalar.activation(sent[m][:].indirect(entries(n3_list, first, count)), h[m][:, cols], ACT.Copy)

        def finish(m):
            result = sbuf(f"result{m}", [P, S], F32)
            pieces = ((0, S, nc.sync),) if m < 3 else ((0, HALF, nc.sync), (HALF, S, nc.scalar))
            for first, last, queue in pieces:
                nc.vector.tensor_tensor(result[:, first:last], h[m][:, first:last], sent[m][:, first:last], ALU.subtract)
                queue.dma_start(out[P * m : P * (m + 1), first:last], result[:, first:last])

        low = gather_dictionary(0)
        make_z(0)
        make_h(0, 0, HALF, "bank4", low)
        make_h(1, 0, HALF, "bank5", low)
        make_z(1)
        make_h(0, HALF, HALF, "bank6", low)
        make_h(1, HALF, HALF, "bank7", low)
        high = gather_dictionary(1)
        finish(0)
        finish(1)
        for m in (2, 3):
            make_h(m, 0, S, f"bank{m}", high)
            finish(m)
